import numpy as np
import ml_dtypes


def mxq(x, axis, fmt="e4m3"):
    dtype, down = {"e4m3": (ml_dtypes.float8_e4m3fn, 7), "e5m2": (ml_dtypes.float8_e5m2, 14)}[fmt]
    v = np.moveaxis(np.asarray(x, np.float32).astype(ml_dtypes.bfloat16).astype(np.float64), axis, -1)
    blocks = v.reshape(v.shape[:-1] + (-1, 32))
    amax = np.abs(blocks).max(-1, keepdims=True)
    byte = np.maximum(np.where(amax > 0, np.frexp(amax)[1] - 1 + 127, 0) - down, 1)
    scale = np.exp2(byte - 127.0)
    codes = (blocks / scale).astype(np.float32).astype(dtype).astype(np.float64)
    return np.moveaxis((codes * scale).reshape(v.shape), -1, axis)


WIDE = False


def mx_kscale(k):
    if not WIDE:
        return np.ones(k)
    levels = np.array([30, -30])
    if k % 512:
        return np.exp2(np.random.permutation(np.resize(levels, k // 32))).repeat(32)
    a = np.empty((k // 512, 16))
    for p in range(k // 512):
        a[p, :8] = np.random.permutation(np.resize(levels, 8))
        for g in range(8):
            far = levels[np.abs(levels - a[p, g]) >= 10]
            a[p, g + 8] = far[np.random.randint(len(far))]
    return np.exp2(a.ravel()).repeat(32)


def f64(x):
    return np.asarray(x).astype(np.float64)


def striped(idx):
    return np.tile(np.asarray(idx).reshape(-1, 16).T, (8, 1)).astype(np.uint16)


def unstriped(offs):
    return offs[:16].T.reshape(-1).astype(np.int64)


E2M1 = np.array([0.0, 0.5, 1.0, 1.5, 2.0, 3.0, 4.0, 6.0, -0.0, -0.5, -1.0, -1.5, -2.0, -3.0, -4.0, -6.0])


def pack_weight(w, fmt):
    k, n = w.shape
    w = f64(np.asarray(w, np.float32).astype(ml_dtypes.bfloat16)).reshape(k // 32, 32, n)
    amax = np.abs(w).max(1)
    if fmt in ("e4m3", "e5m2"):
        byte = np.frexp(amax)[1] - 1 + 127 - (7 if fmt == "e4m3" else 14)
    else:
        mant, ex = np.frexp(amax / 6.0)
        byte = np.where(mant > 0.5, ex, ex - 1) + 127
    byte = np.clip(np.where(amax > 0, byte, 1), 1, 254)
    scaled = (w * np.exp2(127.0 - byte)[:, None, :]).reshape(k, n).astype(np.float32)
    by_word = np.ascontiguousarray(scaled.reshape(k // 512, 128, 4, n).transpose(0, 1, 3, 2))
    if fmt in ("e4m3", "e5m2"):
        words = by_word.astype(ml_dtypes.float8_e4m3fn if fmt == "e4m3" else ml_dtypes.float8_e5m2).view(np.uint8)
    else:
        c = by_word.astype(ml_dtypes.float4_e2m1fn).view(np.uint8) & 0xF
        words = (c[..., 0::2] | (c[..., 1::2] << 4)).reshape(k // 512, 128, 2 * n)
    return np.ascontiguousarray(words), np.ascontiguousarray(byte.astype(np.uint8).reshape(k // 512, 16, n))


def unpack_weight(words, scales, fmt):
    g, _, n = scales.shape
    words = np.ascontiguousarray(words).reshape(g, 128, n, -1)
    if fmt in ("e4m3", "e5m2"):
        vals = words.view(ml_dtypes.float8_e4m3fn if fmt == "e4m3" else ml_dtypes.float8_e5m2).astype(np.float64)
    else:
        nib = np.empty((g, 128, n, 4), np.uint8)
        nib[..., 0::2] = words & 0xF
        nib[..., 1::2] = words >> 4
        vals = E2M1[nib]
    vals = vals * np.repeat(np.exp2(scales.astype(np.float64) - 127.0), 8, axis=1)[..., None]
    return vals.transpose(0, 1, 3, 2).reshape(g * 512, n)


K, T, J, R, V, M, Q, C, O, N, E = 512, 1024, 256, 512, 1024, 512, 128, 512, 128, 256, 1024


def setup_inputs():
    n = np.random.standard_normal
    idx = np.random.permutation(V)[:R]
    idx2 = np.random.permutation(T)[:J]
    idx3 = np.random.permutation(C)[:Q]
    idx4 = np.random.permutation(C)[:O]
    idx5 = np.random.permutation(J)[:O]
    idx6 = np.random.permutation(J)[:O]
    idx7 = np.random.permutation(E)[:O]
    fk = mx_kscale(K)
    fm = mx_kscale(M)
    fr = mx_kscale(R)
    xtp = pack_weight(n((K, T)) / fk[:, None], "e2m1")
    wtp = pack_weight(n((K, V)) * 1 / np.sqrt(K) * fk[:, None], "e4m3")
    xcp = pack_weight(n((M, Q)) / fm[:, None], "e4m3")
    wgp = pack_weight(n((M, R)) * 1 / np.sqrt(M) * fm[:, None] * fr, "e5m2")
    wbp = pack_weight(n((R, N)) * 1 / np.sqrt(R) / fr[:, None], "e2m1")
    return {
        "xt_words": xtp[0],
        "xt_scales": xtp[1],
        "wt_words": wtp[0],
        "wt_scales": wtp[1],
        "xc_words": xcp[0],
        "xc_scales": xcp[1],
        "wg_words": wgp[0],
        "wg_scales": wgp[1],
        "wb_words": wbp[0],
        "wb_scales": wbp[1],
        "offs": striped(idx),
        "offs2": striped(idx2),
        "offs3": striped(idx3),
        "offs4": striped(idx4),
        "offs5": striped(idx5),
        "offs6": striped(idx6),
        "offs7": striped(idx7),
    }


def reference(xt_words, xt_scales, wt_words, wt_scales, xc_words, xc_scales, wg_words, wg_scales, wb_words, wb_scales, offs, offs2, offs3, offs4, offs5, offs6, offs7):
    idx = unstriped(offs)
    idx2 = unstriped(offs2)
    idx3 = unstriped(offs3)
    idx4 = unstriped(offs4)
    idx5 = unstriped(offs5)
    idx6 = unstriped(offs6)
    idx7 = unstriped(offs7)
    xtu = unpack_weight(xt_words, xt_scales, "e2m1")
    wtu = unpack_weight(wt_words, wt_scales, "e4m3")
    xcu = unpack_weight(xc_words, xc_scales, "e4m3")
    wgu = unpack_weight(wg_words, wg_scales, "e5m2")
    wbu = unpack_weight(wb_words, wb_scales, "e2m1")
    wtidxg = wtu[:, idx]
    xtidx2g = xtu[:, idx2]
    a = wtidxg.T @ xtidx2g
    g0 = wgu.T @ xcu
    ga = g0[:, 0:1]
    gb = g0[:, 64:65]
    pw = np.zeros((R, C))
    pw[:, idx3] = g0
    hid = np.maximum(a[:, idx5] * ga, a[:, idx6] * gb) - pw[:, idx4]
    hidq = mxq(hid, 0, "e5m2")
    p = wbu.T @ hidq
    y = np.zeros((N, E))
    y[:, idx7] = p
    return y

from contextlib import ExitStack

import concourse.mybir as mybir
from concourse.masks import make_identity

K, T, J, R, V, M, Q, C, O, N, E = 512, 1024, 256, 512, 1024, 512, 128, 512, 128, 256, 1024
FLOPS = 2 * K * R * J + 2 * M * R * Q + 2 * R * N * O

F32 = mybir.dt.float32
BF16 = mybir.dt.bfloat16
I32 = mybir.dt.int32
U32 = mybir.dt.uint32
U16 = mybir.dt.uint16
U8 = mybir.dt.uint8
E4M3 = mybir.dt.float8_e4m3fn_x4
E5M2 = mybir.dt.float8_e5m2_x4
E2M1 = mybir.dt.float4_e2m1fn_x4
COPY = mybir.ActivationFunctionType.Copy
ALU = mybir.AluOpType

P = 128
PACK = 4
QUADS = 4
QUAD = 32


def tile_list_ctxboard_chosen_one_scattered_kernel(
    tc, xt_words, xt_scales, wt_words, wt_scales, xc_words, xc_scales, wg_words, wg_scales, wb_words, wb_scales,
    offs, offs2, offs3, offs4, offs5, offs6, offs7, out,
):
    nc = tc.nc
    with ExitStack() as ctx:
        lists = ctx.enter_context(tc.tile_pool(name="lists", bufs=1))
        sb = ctx.enter_context(tc.tile_pool(name="sb", bufs=1))
        ps = ctx.enter_context(tc.psum_pool(name="ps", bufs=1))

        def tile(shape, dtype, name, tag=None):
            return sb.tile(shape, dtype, name=name, tag=tag or name, align_bytes=64)

        def load_list(src, name):
            held = lists.tile(list(src.shape), U16, name=name)
            nc.sync.dma_start(held[:], src)
            return held

        def load_words(queue, src, dtype, columns, name):
            held = tile([P, columns], dtype, name)
            queue.dma_start(held[:].bitcast(I32), src.bitcast(I32))
            return held

        def load_rows_side_by_side(src, held):
            nc.sync.dma_start(held[0:PACK], src[0].bitcast(I32).rearrange("(q r) c -> r q c", r=PACK))

        def load_plane(src, plane):
            for q in range(QUADS):
                nc.sync.dma_start(
                    plane[QUAD * q : QUAD * q + PACK, :].bitcast(I32), src[0, PACK * q : PACK * (q + 1), :].bitcast(I32)
                )

        wt_plane = tile([P, V], U8, "wt_plane")
        xt_plane = tile([P, T], U8, "xt_plane")
        nc.vector.memset(xt_plane[:].bitcast(I32), 0)
        nc.vector.memset(wt_plane[:].bitcast(I32), 0)
        boards = [tile([P, C], F32, "board%d" % t) for t in range(PACK)]
        for board in boards:
            nc.vector.memset(board[:], 0.0)
        identity = tile([P, P], F32, "identity")
        make_identity(nc, identity[:])

        gain_rows = tile([P, QUADS, (Q + R) // 4], I32, "gain_rows", tag="then_page1")
        xc_rows, wg_rows = gain_rows[:, :, : Q // 4], gain_rows[:, :, Q // 4 :]
        wt_rows = tile([PACK, QUADS, V // 4], I32, "wt_rows", tag="then_page0")
        load_rows_side_by_side(xc_scales, xc_rows)
        xc_w = load_words(nc.scalar, xc_words[0].rearrange("p n t -> p (n t)"), U32, Q, "xc_w")
        load_rows_side_by_side(wg_scales, wg_rows)
        wg_w = load_words(nc.scalar, wg_words[0].rearrange("p n t -> p (n t)"), U32, R, "wg_w")
        idx = load_list(offs, "idx")
        load_rows_side_by_side(wt_scales, wt_rows)
        idx2 = load_list(offs2, "idx2")
        wt_w = load_words(nc.sync, wt_words[0].rearrange("p n t -> p (n t)"), U32, V, "wt_w")
        load_plane(xt_scales, xt_plane)
        xt_w = load_words(nc.scalar, xt_words[0], U16, T, "xt_w")
        idx3 = load_list(offs3, "idx3")
        idx5 = load_list(offs5, "idx5")
        idx6 = load_list(offs6, "idx6")
        idx4 = load_list(offs4, "idx4")
        idx7 = load_list(offs7, "idx7")
        wb_w = load_words(nc.sync, wb_words[0], U8, 2 * N, "wb_w")
        wb_plane = tile([P, N], U8, "wb_plane")
        load_plane(wb_scales, wb_plane)

        for q in range(1, QUADS):
            nc.vector.tensor_copy(gain_rows[QUAD * q : QUAD * q + PACK, 0, :], gain_rows[0:PACK, q, :])
        for q in range(QUADS):
            nc.vector.tensor_copy(wt_plane[QUAD * q : QUAD * q + PACK, :].bitcast(I32), wt_rows[:, q, :])

        g0_turned_ps = ps.tile([P, R], F32, name="g0_turned_ps", tag="p_ps0")
        nc.tensor.matmul_mx(
            g0_turned_ps[:], lhsT=xc_w[:].bitcast(E4M3), lhsT_scale=xc_rows[:, 0, :].bitcast(U8),
            rhs=wg_w[:].bitcast(E5M2), rhs_scale=wg_rows[:, 0, :].bitcast(U8), start=True, stop=True,
        )
        g0 = []
        for pair in range(2):
            turned = tile([P, 2, P], F32, "g0_turned%d" % pair)
            nc.scalar.copy(turned[:], g0_turned_ps[:].rearrange("q (p t) -> q t p", t=PACK)[:, 2 * pair : 2 * pair + 2, :])
            g0_ps = ps.tile([P, 2, Q], F32, name="g0_ps%d" % pair)
            for u in range(2):
                nc.tensor.transpose(g0_ps[:, u, :], turned[:, u, :], identity[:])
            g0_pair = tile([P, 2, Q], F32, "g0_pair%d" % pair)
            nc.scalar.copy(g0_pair[:], g0_ps[:])
            g0.extend([g0_pair[:, 0, :], g0_pair[:, 1, :]])

        pages = [tile([P, E], F32, "page%d" % h, tag="then_page%d" % h) for h in range(N // P)]
        for page in pages:
            nc.gpsimd.memset(page[:], 0.0)

        wt_picked_plane = tile([P, PACK, P], U8, "wt_picked_plane")
        wt_picked = tile([P, PACK, P], U32, "wt_picked")
        xt_picked_plane = tile([P, J], U8, "xt_picked_plane")
        xt_picked = tile([P, J], U16, "xt_picked")
        nc.vector.tensor_copy(wt_picked_plane[:].rearrange("k t p -> k p t"), wt_plane[:].indirect(idx[:]))
        nc.vector.tensor_copy(wt_picked[:].rearrange("k t p -> k p t"), wt_w[:].indirect(idx[:]))
        nc.vector.tensor_copy(xt_picked_plane[:], xt_plane[:].indirect(idx2[:]))
        nc.vector.tensor_copy(xt_picked[:], xt_w[:].indirect(idx2[:]))

        looked = tile([P, PACK, O], F32, "looked")
        for t in range(3):
            nc.scalar.activation(boards[t][:].indirect(idx3[:]), g0[t], COPY)
        for t in range(2):
            nc.scalar.activation(looked[:, t, :], boards[t][:].indirect(idx4[:]), COPY)

        a = [tile([P, J], F32, "a%d" % t) for t in range(PACK)]
        first = tile([P, PACK, O], F32, "first")
        second = tile([P, PACK, O], F32, "second")
        for t in range(PACK):
            a_ps = ps.tile([P, J], F32, name="a_ps%d" % t)
            nc.tensor.matmul_mx(
                a_ps[:], lhsT=wt_picked[:, t, :].bitcast(E4M3), lhsT_scale=wt_picked_plane[:, t, :],
                rhs=xt_picked[:].bitcast(E2M1), rhs_scale=xt_picked_plane[:], start=True, stop=True,
            )
            nc.vector.tensor_copy(a[t][:], a_ps[:])
            nc.scalar.activation(first[:, t, :], a[t][:].indirect(idx5[:]), COPY, scale=g0[t][:, 0:1])
            nc.scalar.activation(second[:, t, :], a[t][:].indirect(idx6[:]), COPY, scale=g0[t][:, 64:65])

        nc.vector.tensor_copy(boards[3][:].indirect(idx3[:]), g0[3])
        for t in range(2, PACK):
            nc.vector.tensor_copy(looked[:, t, :], boards[t][:].indirect(idx4[:]))

        larger = tile([P, PACK, O], F32, "larger")
        for ts in (slice(0, 2), slice(2, 3), slice(3, 4)):
            nc.vector.tensor_tensor(larger[:, ts, :], first[:, ts, :], second[:, ts, :], ALU.max)
        hid_bf = tile([P, O, PACK], BF16, "hid_bf")
        nc.vector.tensor_tensor(
            hid_bf[:].rearrange("p (c i) t -> p c t i", i=4), larger[:].rearrange("p t (c i) -> p c t i", i=4),
            looked[:].rearrange("p t (c i) -> p c t i", i=4), ALU.subtract,
        )
        hid_words = tile([P, O], U32, "hid_words")
        hid_plane = tile([P, O], U8, "hid_plane")
        nc.vector.quantize_mx(hid_words[:].bitcast(E5M2), hid_plane[:], hid_bf[:].rearrange("p o t -> p (o t)"))

        for h, page in enumerate(pages):
            p_ps = ps.tile([P, O], F32, name="p_ps%d" % h)
            nc.tensor.matmul_mx(
                p_ps[:], lhsT=wb_w[:, 2 * P * h : 2 * P * (h + 1)].bitcast(E2M1), lhsT_scale=wb_plane[:, P * h : P * (h + 1)],
                rhs=hid_words[:].bitcast(E5M2), rhs_scale=hid_plane[:], start=True, stop=True,
            )
            p_sb = tile([P, O], F32, "p_sb%d" % h)
            if h == 0:
                nc.vector.tensor_copy(p_sb[:], p_ps[:])
                nc.vector.tensor_copy(page[:].indirect(idx7[:]), p_sb[:])
                nc.sync.dma_start(out[P * h : P * (h + 1), :], page[:])
            else:
                nc.scalar.copy(p_sb[:], p_ps[:])
                nc.scalar.activation(page[:].indirect(idx7[:]), p_sb[:], COPY)
                nc.scalar.dma_start(out[P * h : P * (h + 1), :], page[:])
